import numpy as np
import ml_dtypes


def mxq(x, axis, fmt="e4m3"):
    dtype, down = {"e4m3": (ml_dtypes.float8_e4m3fn, 7), "e5m2": (ml_dtypes.float8_e5m2, 14)}[fmt]
    v = np.moveaxis(np.asarray(x, np.float32).astype(ml_dtypes.bfloat16).astype(np.float64), axis, -1)
    blocks = v.reshape(v.shape[:-1] + (-1, 32))
    amax = np.abs(blocks).max(-1, keepdims=True)
    byte = np.maximum(np.where(amax > 0, np.frexp(amax)[1] - 1 + 127, 0) - down, 1)
    scale = np.exp2(byte - 127.0)
    codes = (blocks / scale).astype(np.float32).astype(dtype).astype(np.float64)
    return np.moveaxis((codes * scale).reshape(v.shape), -1, axis)


WIDE = False


def mx_kscale(k):
    if not WIDE:
        return np.ones(k)
    levels = np.array([10, -10, 5, -5, 0])
    if k % 512:
        return np.exp2(np.random.permutation(np.resize(levels, k // 32))).repeat(32)
    a = np.empty((k // 512, 16))
    for p in range(k // 512):
        a[p, :8] = np.random.permutation(np.resize(levels, 8))
        for g in range(8):
            far = levels[np.abs(levels - a[p, g]) >= 10]
            a[p, g + 8] = far[np.random.randint(len(far))]
    return np.exp2(a.ravel()).repeat(32)


def f64(x):
    return np.asarray(x).astype(np.float64)


def striped(idx):
    return np.tile(idx.reshape(-1, 16).T, (8, 1)).astype(np.uint16)


def unstriped(offs):
    return offs[:16].T.reshape(-1).astype(np.int64)


def pack_weight(w):
    k, n = w.shape
    w = f64(np.asarray(w, np.float32).astype(ml_dtypes.bfloat16)).reshape(k // 32, 32, n)
    amax = np.abs(w).max(1)
    byte = np.clip(np.where(amax > 0, np.frexp(amax)[1] - 1 + 127 - 7, 1), 1, 254)
    scaled = (w * np.exp2(127.0 - byte)[:, None, :]).reshape(k, n).astype(np.float32)
    words = np.ascontiguousarray(scaled.reshape(k // 512, 128, 4, n).transpose(0, 1, 3, 2)).astype(ml_dtypes.float8_e4m3fn).view(np.uint8)
    return words, np.ascontiguousarray(byte.astype(np.uint8).reshape(k // 512, 16, n))


def unpack_weight(words, scales):
    g, p, n, _ = words.shape
    vals = np.ascontiguousarray(words).view(ml_dtypes.float8_e4m3fn).astype(np.float64) * np.repeat(np.exp2(scales.astype(np.float64) - 127.0), 8, axis=1)[..., None]
    return vals.transpose(0, 1, 3, 2).reshape(g * 512, n)


def silu(v):
    return v / (1.0 + np.exp(-np.maximum(v, -700.0)))


K, T, S, D, H, N, V, W, R = 512, 1024, 512, 2, 512, 128, 256, 1024, 256
P = 2 ** 7


def setup_inputs():
    n = np.random.standard_normal
    s = mx_kscale(K)[:, None]
    u = mx_kscale(H)
    packed_xT = pack_weight(n((K, T)) * s)
    packed_eT = pack_weight(n((K, W)) * s)
    return {
        "x_words": packed_xT[0],
        "x_scales": packed_xT[1],
        "e_words": packed_eT[0],
        "e_scales": packed_eT[1],
        "w1": (n((K, H)) / np.sqrt(K) / s * u).astype(np.float32),
        "w2": (n((K, H)) / np.sqrt(K) / s).astype(np.float32),
        "w3": (n((H, N)) / np.sqrt(H) / u[:, None]).astype(np.float32),
        "dirx": (np.tile(n(S) / np.sqrt(3), (P, 1))).astype(np.float32),
        "diry": (np.tile(n(S) / np.sqrt(3), (P, 1))).astype(np.float32),
        "co0": (np.random.uniform(-1.0, 1.0, (H, R))).astype(np.float32),
        "co1": (np.random.uniform(-1.0, 1.0, (H, R))).astype(np.float32),
        "co2": (np.random.uniform(-1.0, 1.0, (H, R))).astype(np.float32),
        "unit": (1.0 / u[:, None] * np.random.uniform(0.8, 1.2, (H, 1))).astype(np.float32),
        "offs": striped(np.random.permutation(T)[:S]),
        "dbin": striped(np.random.permutation(W)[:S]),
        "el": striped(np.random.randint(0, R, V)),
    }


def reference(x_words, x_scales, e_words, e_scales, w1, w2, w3, dirx, diry, co0, co1, co2, unit, offs, dbin, el):
    xq = unpack_weight(x_words, x_scales)[:, unstriped(offs)]
    y = mxq(f64(w1), 0, "e4m3").T @ xq
    e_dbin = unpack_weight(e_words, e_scales)[:, unstriped(dbin)]
    h = y * ((mxq(f64(w2), 0, "e4m3").T @ e_dbin))
    a0 = h.reshape(len(h), -1, D).mean(axis=2)
    gx = h * f64(dirx)[:1]
    ax = gx.reshape(len(gx), -1, D).mean(axis=2)
    gy = h * f64(diry)[:1]
    ay = gy.reshape(len(gy), -1, D).mean(axis=2)
    nn = f64(unit) * (ax * ax + ay * ay)
    z = f64(co0)[:, unstriped(el)] * a0 + f64(co1)[:, unstriped(el)] * (a0 * (f64(unit) * a0)) + f64(co2)[:, unstriped(el)] * nn
    return silu(mxq(f64(w3), 0, "e4m3").T @ mxq(z, 0, "e4m3"))

from contextlib import ExitStack

import concourse.mybir as mybir
from concourse.masks import make_identity

F32 = mybir.dt.float32
BF16 = mybir.dt.bfloat16
I32 = mybir.dt.int32
U32 = mybir.dt.uint32
U16 = mybir.dt.uint16
U8 = mybir.dt.uint8
FP8X4 = mybir.dt.float8_e4m3fn_x4
ACT = mybir.ActivationFunctionType
ALU = mybir.AluOpType

P = 128
PACK = 4
K, T, S, H, N, V, R = 512, 1024, 512, 512, 128, 256, 256
HALF = H // 2
FLOPS = 2 * K * H * S * 2 + 2 * H * N * V


def tile_picked_yace_silu_p_kernel(
    tc, x_words, x_scales, e_words, e_scales, w1, w2, w3, dirx, diry, co0, co1, co2, unit, offs, dbin, el, out
):
    nc = tc.nc
    with ExitStack() as ctx:
        pool = ctx.enter_context(tc.tile_pool(name="keep", bufs=1))
        psum = ctx.enter_context(tc.psum_pool(name="psum", bufs=8))

        def tile(shape, dtype, name):
            return pool.tile(shape, dtype, name=name, align_bytes=64)

        def bank(name):
            return psum.tile([P, 512], F32, name=name, tag="bank")

        offs_t = pool.tile([P, S // 16], U16, name="offs_t")
        dbin_t = pool.tile([P, S // 16], U16, name="dbin_t")
        el_t = pool.tile([P, V // 16], U16, name="el_t")

        xw = tile([P, T], U32, "xw")
        ew = tile([P, T], U32, "ew")
        xs = tile([P, T], U8, "xs")
        es = tile([P, T], U8, "es")

        nc.vector.memset(xs[:].bitcast(I32), 0)
        nc.vector.memset(es[:].bitcast(I32), 0)

        def load_scales(dst, src):
            for q in range(4):
                nc.sync.dma_start(dst[32 * q : 32 * q + 4, :].bitcast(I32), src[0, 4 * q : 4 * q + 4, :].bitcast(I32))

        def load_words(dst, src):
            nc.sync.dma_start(dst[:].bitcast(I32), src[0].rearrange("p n t -> p (n t)").bitcast(I32))

        dx = tile([P, 2, 2], F32, "dx")
        dy = tile([P, 2, 2], F32, "dy")
        un = tile([P, PACK], F32, "un")
        nc.gpsimd.dma_start(dx[:], dirx[0].rearrange("(g p e) -> p g e", p=P, e=2))
        nc.gpsimd.dma_start(dy[:], diry[0].rearrange("(g p e) -> p g e", p=P, e=2))
        nc.gpsimd.dma_start(un[:], unit.rearrange("(p t) o -> p (t o)", t=PACK))

        nc.sync.dma_start(offs_t[:], offs)
        load_scales(xs, x_scales)
        load_words(xw, x_words)
        nc.sync.dma_start(dbin_t[:], dbin)
        load_words(ew, e_words)
        load_scales(es, e_scales)

        raw = {}
        for name, w in (("w1", w1), ("w2", w2)):
            for c in range(2):
                raw[name, c] = tile([P, PACK, HALF], F32, "raw_%s_%d" % (name, c))
                nc.sync.dma_start(
                    raw[name, c][:], w[:, c * HALF : (c + 1) * HALF].rearrange("(p j) n -> p j n", j=PACK)
                )
        nc.sync.dma_start(el_t[:], el)
        co = {}
        for b, src in ((1, co1), (0, co0), (2, co2)):
            rows = src.rearrange("(p t) r -> p t r", t=PACK)
            for t in range(PACK):
                co[b, t] = tile([P, R], F32, "co%d_%d" % (b, t))
                nc.sync.dma_start(co[b, t][:], rows[:, t, :])
        raw3 = tile([P, PACK, N], F32, "raw3")
        nc.sync.dma_start(raw3[:], w3.rearrange("(p j) n -> p j n", j=PACK))

        half = tile([P, 4], F32, "half")
        nc.gpsimd.memset(half[:], 0.5)
        warm = tile([P, 1], F32, "warm")
        nc.scalar.activation(warm[:], half[:, 0:1], ACT.Silu)
        ident = tile([P, P], F32, "ident")
        make_identity(nc, ident[:])

        sqx = tile([P, 2, 2], F32, "sqx")
        sqy = tile([P, 2, 2], F32, "sqy")
        norm2 = tile([P, 2, 2], F32, "norm2")
        norm = tile([P, 2, 2], F32, "norm")
        px = tile([P, 2], F32, "px")
        py = tile([P, 2], F32, "py")
        dot = tile([P, 2], F32, "dot")
        dot2 = tile([P, 2], F32, "dot2")
        nc.gpsimd.tensor_tensor(sqx[:], dx[:], dx[:], ALU.mult)
        nc.gpsimd.tensor_tensor(sqy[:], dy[:], dy[:], ALU.mult)
        nc.gpsimd.tensor_tensor(norm2[:], sqx[:], sqy[:], ALU.add)
        nc.gpsimd.tensor_tensor(norm[:].rearrange("p g e -> p (g e)"), norm2[:].rearrange("p g e -> p (g e)"), half[:], ALU.pow)
        nc.gpsimd.tensor_tensor(px[:], dx[:, :, 0], dx[:, :, 1], ALU.mult)
        nc.gpsimd.tensor_tensor(py[:], dy[:, :, 0], dy[:, :, 1], ALU.mult)
        nc.gpsimd.tensor_tensor(dot[:], px[:], py[:], ALU.add)
        nc.gpsimd.tensor_tensor(dot2[:], dot[:], dot[:], ALU.add)

        def pick(src, idx, dtype, name):
            got = tile([P, S], dtype, name + "_got")
            nc.vector.tensor_copy(got[:], src[:].indirect(idx[:]))
            return got

        def deal(got, dtype, name):
            dealt = tile([P, 2, V], dtype, name + "_dealt")
            nc.vector.tensor_copy(dealt[:], got[:].rearrange("p (v e) -> p e v", e=2))
            return dealt

        def cast(engine, src, width, name):
            grouped = tile([P, width, PACK], BF16, name)
            dst_view = grouped[:].rearrange("p (c i) j -> p c j i", i=4)
            src_view = src[:].rearrange("p j (c i) -> p c j i", i=4)
            if engine == "scalar":
                nc.scalar.copy(dst_view, src_view)
            else:
                nc.vector.tensor_copy(dst_view, src_view)
            return grouped

        def quantise(codes, scales, grouped):
            nc.vector.quantize_mx(out=codes.bitcast(FP8X4), scales=scales, in_=grouped.rearrange("p n j -> p (n j)"))

        xs_g = pick(xs, offs_t, U8, "xs")
        xw_g = pick(xw, offs_t, U32, "xw")
        xs_d = deal(xs_g, U8, "xs")
        xw_d = deal(xw_g, U32, "xw")
        ew_g = pick(ew, dbin_t, U32, "ew")
        es_g = pick(es, dbin_t, U8, "es")
        ew_d = deal(ew_g, U32, "ew")
        es_d = deal(es_g, U8, "es")

        codes = {n: tile([P, H], U32, n + "_codes") for n in ("w1", "w2")}
        planes = {n: tile([P, H], U8, n + "_scales") for n in ("w1", "w2")}
        grouped = {}
        for name, c, engine in (("w1", 0, "scalar"), ("w1", 1, "scalar"), ("w2", 0, "scalar"), ("w2", 1, "vector")):
            grouped[name, c] = cast(engine, raw[name, c], HALF, "bf_%s_%d" % (name, c))
        for name in ("w1", "w2"):
            for c in range(2):
                cols = slice(c * HALF, (c + 1) * HALF)
                quantise(codes[name][:, cols], planes[name][:, cols], grouped[name, c][:])

        def product(words, scales, name, g, e):
            acc = bank("acc_%s_%d%d" % (name, g, e))
            cols = slice(g * P, (g + 1) * P)
            nc.tensor.matmul_mx(
                out=acc[:],
                lhsT=words[:, e, cols].bitcast(FP8X4),
                lhsT_scale=scales[:, e, cols],
                rhs=codes[name][:].bitcast(FP8X4),
                rhs_scale=planes[name][:],
                start=True,
                stop=True,
            )
            return acc

        def by_tile(acc):
            return acc[:].rearrange("p (m t) -> p t m", t=PACK)

        pairs = [(g, e) for g in range(2) for e in range(2)]
        yh = {}
        for g, e in pairs:
            acc = product(xw_d, xs_d, "w1", g, e)
            yh[g, e] = tile([P, PACK, P], F32, "yh%d%d" % (g, e))
            nc.scalar.activation(yh[g, e][:], by_tile(acc), ACT.Copy, scale=0.5)

        def turn_and_add(terms, name):
            acc = bank(name)
            for t in range(PACK):
                for n, term in enumerate(terms):
                    nc.tensor.matmul(
                        acc[:, t * P : (t + 1) * P], term[:, t, :], ident[:],
                        start=(n == 0), stop=(n == len(terms) - 1), is_transpose=True,
                    )
            return acc

        def times_unit(acc, name):
            res = tile([P, PACK, P], F32, name)
            for t in range(PACK):
                nc.scalar.activation(res[:, t, :], acc[:, t * P : (t + 1) * P], ACT.Copy, scale=un[:, t : t + 1])
            return res

        h, a0, ua0, cross, sq = {}, {}, {}, {}, {}
        for g in range(2):
            for e in range(2):
                acc = product(ew_d, es_d, "w2", g, e)
                h[g, e] = tile([P, PACK, P], F32, "h%d%d" % (g, e))
                nc.vector.tensor_tensor(h[g, e][:], by_tile(acc), yh[g, e][:], ALU.mult)
            a0[g] = turn_and_add([h[g, 0], h[g, 1]], "a0_%d" % g)
            ua0[g] = times_unit(a0[g], "ua0_%d" % g)
        for g in range(2):
            cross[g] = tile([P, PACK, P], F32, "cross%d" % g)
            nc.vector.scalar_tensor_tensor(
                cross[g][:].rearrange("p t m -> p (t m)"), h[g, 0][:].rearrange("p t m -> p (t m)"),
                dot2[:, g : g + 1], h[g, 1][:].rearrange("p t m -> p (t m)"), ALU.mult, ALU.mult,
            )
        unn = {}
        for g in range(2):
            for e in range(2):
                sq[g, e] = tile([P, PACK, P], F32, "sq%d%d" % (g, e))
                nc.scalar.activation(sq[g, e][:], h[g, e][:], ACT.Square, scale=norm[:, g, e : e + 1])
            nn = turn_and_add([cross[g], sq[g, 0], sq[g, 1]], "nn_%d" % g)
            unn[g] = times_unit(nn, "unn_%d" % g)

        def looked_up(b, g, other, op, name):
            res = tile([P, PACK, P], F32, name)
            entries = el_t[:, g * (P // 16) : (g + 1) * (P // 16)]
            for t in range(PACK):
                nc.vector.tensor_tensor(res[:, t, :], co[b, t][:].indirect(entries), other[:, t, :], op)
            return res

        lin, quad = {}, {}
        inner = {}
        for g in range(2):
            first = looked_up(1, g, ua0[g], ALU.mult, "first%d" % g)
            inner[g] = looked_up(0, g, first, ALU.add, "inner%d" % g)
        for g in range(2):
            lin[g] = tile([P, PACK, P], F32, "lin%d" % g)
            nc.vector.tensor_tensor(lin[g][:].rearrange("p t v -> p (t v)"), inner[g][:].rearrange("p t v -> p (t v)"), a0[g][:], ALU.mult)

        w3_bf = cast("scalar", raw3, N, "bf_w3")
        w3_codes = tile([P, N], U32, "w3_codes")
        w3_scales = tile([P, N], U8, "w3_scales")
        quantise(w3_codes[:], w3_scales[:], w3_bf[:])

        for g in range(2):
            quad[g] = looked_up(2, g, unn[g], ALU.mult, "quad%d" % g)
        for g in range(2):
            z = tile([P, P, PACK], BF16, "z%d" % g)
            nc.vector.tensor_tensor(
                z[:].rearrange("p (c i) t -> p c t i", i=4),
                lin[g][:].rearrange("p t (c i) -> p c t i", i=4),
                quad[g][:].rearrange("p t (c i) -> p c t i", i=4),
                ALU.add,
            )
            z_codes = tile([P, P], U32, "z_codes%d" % g)
            z_scales = tile([P, P], U8, "z_scales%d" % g)
            quantise(z_codes[:], z_scales[:], z[:])
            acc = bank("res%d" % g)
            nc.tensor.matmul_mx(
                out=acc[:, 0:P], lhsT=w3_codes[:].bitcast(FP8X4), lhsT_scale=w3_scales[:],
                rhs=z_codes[:].bitcast(FP8X4), rhs_scale=z_scales[:], start=True, stop=True,
            )
            res = tile([P, P], F32, "res_sb%d" % g)
            nc.scalar.activation(res[:], acc[:, 0:P], ACT.Silu)
            nc.sync.dma_start(out[:, g * P : (g + 1) * P], res[:])
